import numpy as np
import ml_dtypes


def mxq(x, axis, fmt="e4m3"):
    dtype, down = {"e4m3": (ml_dtypes.float8_e4m3fn, 7), "e5m2": (ml_dtypes.float8_e5m2, 14)}[fmt]
    v = np.moveaxis(np.asarray(x, np.float32).astype(ml_dtypes.bfloat16).astype(np.float64), axis, -1)
    blocks = v.reshape(v.shape[:-1] + (-1, 32))
    amax = np.abs(blocks).max(-1, keepdims=True)
    byte = np.maximum(np.where(amax > 0, np.frexp(amax)[1] - 1 + 127, 0) - down, 1)
    scale = np.exp2(byte - 127.0)
    codes = (blocks / scale).astype(np.float32).astype(dtype).astype(np.float64)
    return np.moveaxis((codes * scale).reshape(v.shape), -1, axis)


WIDE = False


def mx_kscale(k):
    if not WIDE:
        return np.ones(k)
    levels = np.array([10, -10, 5, -5, 0])
    if k % 512:
        return np.exp2(np.random.permutation(np.resize(levels, k // 32))).repeat(32)
    a = np.empty((k // 512, 16))
    for p in range(k // 512):
        a[p, :8] = np.random.permutation(np.resize(levels, 8))
        for g in range(8):
            far = levels[np.abs(levels - a[p, g]) >= 10]
            a[p, g + 8] = far[np.random.randint(len(far))]
    return np.exp2(a.ravel()).repeat(32)


def f64(x):
    return np.asarray(x).astype(np.float64)


def striped(idx):
    return np.tile(np.asarray(idx).reshape(-1, 16).T, (8, 1)).astype(np.uint16)


def unstriped(offs):
    return offs[:16].T.reshape(-1).astype(np.int64)


E2M1 = np.array([0.0, 0.5, 1.0, 1.5, 2.0, 3.0, 4.0, 6.0, -0.0, -0.5, -1.0, -1.5, -2.0, -3.0, -4.0, -6.0])


def pack_weight(w, fmt):
    k, n = w.shape
    w = f64(np.asarray(w, np.float32).astype(ml_dtypes.bfloat16)).reshape(k // 32, 32, n)
    amax = np.abs(w).max(1)
    if fmt == "e4m3":
        byte = np.frexp(amax)[1] - 1 + 127 - 7
    else:
        mant, ex = np.frexp(amax / 6.0)
        byte = np.where(mant > 0.5, ex, ex - 1) + 127
    byte = np.clip(np.where(amax > 0, byte, 1), 1, 254)
    scaled = (w * np.exp2(127.0 - byte)[:, None, :]).reshape(k, n).astype(np.float32)
    by_word = np.ascontiguousarray(scaled.reshape(k // 512, 128, 4, n).transpose(0, 1, 3, 2))
    if fmt == "e4m3":
        words = by_word.astype(ml_dtypes.float8_e4m3fn).view(np.uint8)
    else:
        c = by_word.astype(ml_dtypes.float4_e2m1fn).view(np.uint8) & 0xF
        words = (c[..., 0::2] | (c[..., 1::2] << 4)).reshape(k // 512, 128, 2 * n)
    return np.ascontiguousarray(words), np.ascontiguousarray(byte.astype(np.uint8).reshape(k // 512, 16, n))


def unpack_weight(words, scales, fmt):
    g, _, n = scales.shape
    words = np.ascontiguousarray(words).reshape(g, 128, n, -1)
    if fmt == "e4m3":
        vals = words.view(ml_dtypes.float8_e4m3fn).astype(np.float64)
    else:
        nib = np.empty((g, 128, n, 4), np.uint8)
        nib[..., 0::2] = words & 0xF
        nib[..., 1::2] = words >> 4
        vals = E2M1[nib]
    vals = vals * np.repeat(np.exp2(scales.astype(np.float64) - 127.0), 8, axis=1)[..., None]
    return vals.transpose(0, 1, 3, 2).reshape(g * 512, n)


D, T, I, Q, E, G = 512, 2048, 512, 256, 512, 8


def setup_inputs():
    n = np.random.standard_normal
    idx = np.random.permutation(T)[:I]
    fd = mx_kscale(D)
    fi = mx_kscale(I)
    ti = np.ones(T)
    ti[idx] = fi
    keysp = pack_weight(n((D, T)) / fd[:, None], "e4m3")
    return {
        "query": (n((D, Q)) * 0.5 / np.sqrt(D) * fd[:, None]).astype(np.float32),
        "keys_words": keysp[0],
        "keys_scales": keysp[1],
        "size": (np.random.uniform(0.5, 2.0, (1, I)) * fi).astype(np.float32),
        "vals": (n((E, T)) / ti).astype(np.float32),
        "target": (n((Q, E)) * 0.06).astype(np.float32),
        "fw": (np.random.uniform(0.3, 1.5, (1, E))).astype(np.float32),
        "tol": (0.2 * n((Q, G))).astype(np.float32),
        "offs": striped(idx),
    }


def reference(query, keys_words, keys_scales, size, vals, target, fw, tol, offs):
    idx = unstriped(offs)
    keysu = unpack_weight(keys_words, keys_scales, "e4m3")
    queryq = mxq(f64(query), 0, "e4m3")
    keysidxg = keysu[:, idx]
    a = queryq.T @ keysidxg
    p = np.exp(a - np.max(a, axis=1, keepdims=True))
    w = p * f64(size) / np.sum(p, axis=1, keepdims=True)
    wt = w.T
    vt = f64(vals)[:, idx].T
    wtq = mxq(wt, 0, "e4m3")
    vtq = mxq(vt, 0, "e4m3")
    o = wtq.T @ vtq
    y = np.sqrt((np.square(o - f64(target)) * f64(fw)).reshape(Q, G, E // G).mean(axis=2)) * 16.0 - f64(tol)
    return y

@@ -1,0 +1,216 @@
+from contextlib import ExitStack
+
+import concourse.mybir as mybir
+from concourse.masks import make_identity
+
+D, T, I, Q, E, G = 512, 2048, 512, 256, 512, 8
+FLOPS = 2 * Q * I * D + 2 * Q * E * I
+
+F32 = mybir.dt.float32
+BF16 = mybir.dt.bfloat16
+I32 = mybir.dt.int32
+U32 = mybir.dt.uint32
+U16 = mybir.dt.uint16
+U8 = mybir.dt.uint8
+FP8X4 = mybir.dt.float8_e4m3fn_x4
+ALU = mybir.AluOpType
+ACT = mybir.ActivationFunctionType
+AXIS = mybir.AxisListType
+
+P = 128
+PACK = 4
+HALVES = Q // P
+CHUNKS = E // P
+BLOCK = E // G
+EARLY = (CHUNKS - 1) * P
+
+
+def tile_attend_readerrors_kernel(tc, query, keys_words, keys_scales, size, vals, target, fw, tol, offs, out):
+    nc = tc.nc
+    with ExitStack() as ctx:
+        keep = ctx.enter_context(tc.tile_pool(name="keep", bufs=1))
+        work = ctx.enter_context(tc.tile_pool(name="work", bufs=2))
+        psum = ctx.enter_context(tc.psum_pool(name="psum", bufs=1))
+
+        offsets = keep.tile([P, I // 16], U16, name="offsets")
+        nc.sync.dma_start(offsets[:], offs)
+
+        key_scales = keep.tile([P, T], U8, name="key_scales", align_bytes=64)
+        nc.gpsimd.memset(key_scales[:].bitcast(I32), 0)
+        ident = keep.tile([P, P], F32, name="ident")
+        make_identity(nc, ident[:])
+
+        q_raw = keep.tile([P, PACK, Q], F32, name="q_raw")
+        nc.sync.dma_start(q_raw[:], query.rearrange("(p j) q -> p j q", j=PACK))
+        for quad in range(4):
+            nc.sync.dma_start(
+                key_scales[32 * quad : 32 * quad + 4, :].bitcast(I32),
+                keys_scales[0, 4 * quad : 4 * quad + 4, :].bitcast(I32),
+            )
+        size_sb = keep.tile([P, PACK], F32, name="size_sb")
+        nc.sync.dma_start(size_sb[:], size.rearrange("o (p t) -> p (o t)", t=PACK))
+        key_words = keep.tile([P, T], U32, name="key_words", align_bytes=64)
+        nc.sync.dma_start(key_words[:].bitcast(I32), keys_words[0].rearrange("p n t -> p (n t)").bitcast(I32))
+
+        val_rows = [keep.tile([P, T], F32, name="val_rows%d" % c, tag="val%d" % c, align_bytes=64) for c in range(CHUNKS)]
+        target_rows = target.rearrange("(h p) e -> p h e", p=P)
+        target_sb = [keep.tile([P, HALVES, E // 2], F32, name="target%d" % k) for k in range(2)]
+        fw_sb = keep.tile([P, PACK], F32, name="fw_sb")
+        tol_sb = keep.tile([P, HALVES, G], F32, name="tol_sb")
+        nc.sync.dma_start(val_rows[0][:], vals[0:P, :])
+        nc.sync.dma_start(fw_sb[:], fw.rearrange("o (p t) -> p (o t)", t=PACK))
+        nc.sync.dma_start(val_rows[1][:], vals[P : 2 * P, :])
+        nc.sync.dma_start(tol_sb[:], tol.rearrange("(h p) g -> p h g", p=P))
+        nc.sync.dma_start(val_rows[2][:], vals[2 * P : 3 * P, :])
+        nc.sync.dma_start(target_sb[0][:], target_rows[:, :, 0 : E // 2])
+        nc.sync.dma_start(val_rows[3][:], vals[3 * P : 4 * P, :])
+        nc.sync.dma_start(target_sb[1][:], target_rows[:, :, E // 2 : E])
+
+        q_grouped = keep.tile([P, Q, PACK], BF16, name="q_grouped", align_bytes=64)
+        nc.scalar.activation(
+            q_grouped[:].rearrange("p (c i) t -> p c t i", i=4),
+            q_raw[:].rearrange("p t (c i) -> p c t i", i=4),
+            ACT.Copy,
+        )
+        q_codes = keep.tile([P, Q], U32, name="q_codes", align_bytes=64)
+        q_scales = keep.tile([P, Q], U8, name="q_scales", align_bytes=64)
+        nc.vector.quantize_mx(q_codes[:].bitcast(FP8X4), q_scales[:], q_grouped[:].rearrange("p q t -> p (q t)"))
+
+        k_scales = keep.tile([P, I], U8, name="k_scales", align_bytes=64)
+        nc.vector.tensor_copy(k_scales[:], key_scales[:].indirect(offsets[:]))
+        k_codes = keep.tile([P, I], U32, name="k_codes", align_bytes=64)
+        nc.vector.tensor_copy(k_codes[:], key_words[:].indirect(offsets[:]))
+
+        size_bank = psum.tile([P, PACK, P], F32, name="size_bank")
+        fw_bank = psum.tile([P, PACK, P], F32, name="fw_bank")
+        for t in range(PACK):
+            nc.tensor.transpose(size_bank[:, t, :], size_sb[:, t : t + 1].to_broadcast([P, P]), ident[:])
+        size_row = size_bank[:].rearrange("c t p -> c p t")
+        fw_row = fw_bank[:].rearrange("c t p -> c p t")
+
+        def turn_and_quantize(rows, name, grouped_tag, codes_tag):
+            n = len(rows)
+            turned = psum.tile([P, n, 2, P], F32, name="turned", tag="turned", bufs=3)
+            for k in range(n):
+                words = rows[k][:].bitcast(F32)
+                for u in range(2):
+                    nc.tensor.transpose(turned[:, k, u, :], words[:, u : I // 2 : 2], ident[:])
+            grouped = keep.tile([P, n * P * PACK], BF16, name=name + "_grouped", tag=grouped_tag, align_bytes=64)
+            nc.scalar.copy(
+                grouped[:].bitcast(F32).rearrange("p (k r u) -> p k r u", k=n, u=2),
+                turned[:].rearrange("p k u r -> p k r u"),
+            )
+            codes = keep.tile([P, n * P], U32, name=name + "_codes", tag=codes_tag, align_bytes=64)
+            scales = keep.tile([P, n * P], U8, name=name + "_scales", align_bytes=64)
+            nc.vector.quantize_mx(codes[:].bitcast(FP8X4), scales[:], grouped[:])
+            return codes, scales
+
+        v_rows = [keep.tile([P, I], BF16, name="v_rows%d" % c) for c in range(CHUNKS)]
+        nc.scalar.activation(v_rows[0][:], val_rows[0][:].indirect(offsets[:]), ACT.Copy)
+
+        w_rows = []
+        for h in range(HALVES):
+            cols = slice(h * P, (h + 1) * P)
+            scores = psum.tile([P, I], F32, name="scores", tag="sums", bufs=3)
+            nc.tensor.matmul_mx(
+                out=scores[:],
+                lhsT=q_codes[:, cols].bitcast(FP8X4),
+                lhsT_scale=q_scales[:, cols],
+                rhs=k_codes[:].bitcast(FP8X4),
+                rhs_scale=k_scales[:],
+                start=True,
+                stop=True,
+            )
+            neg_max = work.tile([P, 1], F32, name="neg_max")
+            nc.vector.tensor_reduce(neg_max[:], scores[:], AXIS.X, ALU.max, negate=True)
+            probs = keep.tile([P, I], F32, name="probs%d" % h, tag="val0" if h == 0 else "probs", align_bytes=64)
+            row_sum = work.tile([P, 1], F32, name="row_sum")
+            nc.scalar.activation(probs[:], scores[:], ACT.Exp, bias=neg_max[:], scale=1.0, accum_out=row_sum[:])
+            inv_sum = work.tile([P, 1], F32, name="inv_sum")
+            nc.vector.reciprocal(inv_sum[:], row_sum[:])
+            w_half = work.tile([P, I], BF16, name="w_half")
+            nc.vector.scalar_tensor_tensor(
+                w_half[:].rearrange("q (p t) -> q p t", t=PACK),
+                probs[:].rearrange("q (p t) -> q p t", t=PACK),
+                inv_sum[:],
+                size_row,
+                ALU.mult,
+                ALU.mult,
+            )
+            w_rows.append(w_half)
+
+        nc.scalar.activation(v_rows[1][:], val_rows[1][:].indirect(offsets[:]), ACT.Copy)
+        nc.vector.tensor_copy(v_rows[2][:], val_rows[2][:].indirect(offsets[:]))
+        w_codes, w_scales = turn_and_quantize(w_rows, "w", "val1", "val2")
+        for t in range(PACK):
+            nc.tensor.transpose(fw_bank[:, t, :], fw_sb[:, t : t + 1].to_broadcast([P, P]), ident[:])
+
+        def read_values(chunks):
+            name = "v%d" % chunks[0]
+            v_codes, v_scales = turn_and_quantize([v_rows[c] for c in chunks], name, name + "g", name + "c")
+            reads = psum.tile([P, HALVES, len(chunks) * P], F32, name="reads", tag="sums", bufs=3)
+            for h in range(HALVES):
+                cols = slice(h * P, (h + 1) * P)
+                nc.tensor.matmul_mx(
+                    out=reads[:, h, :],
+                    lhsT=w_codes[:, cols].bitcast(FP8X4),
+                    lhsT_scale=w_scales[:, cols],
+                    rhs=v_codes[:].bitcast(FP8X4),
+                    rhs_scale=v_scales[:],
+                    start=True,
+                    stop=True,
+                )
+            return reads
+
+        sums = keep.tile([P, HALVES, G], F32, name="sums")
+
+        def by_place(ap):
+            return ap.rearrange("q (p t) -> q p t", t=PACK)
+
+        def fw_at(first, width):
+            return fw_row[:, first // PACK : (first + width) // PACK, :]
+
+        def sum_errors(reads, wanted, first, width, diff_tag):
+            diff = keep.tile([P, HALVES, width], F32, name="diff%d" % first, tag=diff_tag, align_bytes=64)
+            nc.vector.tensor_tensor(diff[:], reads[:], wanted, ALU.subtract)
+            squares = keep.tile([P, HALVES, width], F32, name="squares%d" % first)
+            nc.scalar.activation(squares[:], diff[:], ACT.Square)
+            for h in range(HALVES):
+                for e in range(0, width, BLOCK):
+                    g = (first + e) // BLOCK
+                    block = by_place(squares[:, h, e : e + BLOCK])
+                    nc.vector.scalar_tensor_tensor(
+                        block, block, 256.0 / BLOCK, fw_at(first + e, BLOCK), ALU.mult, ALU.mult,
+                        accum_out=sums[:, h, g : g + 1],
+                    )
+
+        def sum_errors_on_vector(reads, wanted, first, width):
+            diff = keep.tile([P, HALVES, width], F32, name="diff_last")
+            weighted = keep.tile([P, HALVES, width], F32, name="weighted")
+            for h in range(HALVES):
+                nc.vector.tensor_tensor(diff[:, h, :], reads[:, h, :], wanted[:, h, :], ALU.subtract)
+            for h in range(HALVES):
+                nc.vector.tensor_tensor(by_place(weighted[:, h, :]), by_place(diff[:, h, :]), fw_at(first, width), ALU.mult)
+            for h in range(HALVES):
+                for e in range(0, width, BLOCK):
+                    g = (first + e) // BLOCK
+                    block = weighted[:, h, e : e + BLOCK]
+                    nc.vector.scalar_tensor_tensor(
+                        block, block, 256.0 / BLOCK, diff[:, h, e : e + BLOCK], ALU.mult, ALU.mult,
+                        accum_out=sums[:, h, g : g + 1],
+                    )
+
+        reads01 = read_values([0, 1])
+        reads2 = read_values([2])
+        nc.scalar.activation(v_rows[3][:, 0 : I // 2], val_rows[3][:].indirect(offsets[:, 0 : I // 32]), ACT.Copy)
+        nc.vector.tensor_copy(v_rows[3][:, I // 2 : I], val_rows[3][:].indirect(offsets[:, I // 32 : I // 16]))
+        reads3 = read_values([3])
+        sum_errors(reads01, target_sb[0][:], 0, 2 * P, "val3")
+        sum_errors(reads2, target_sb[1][:, :, 0:P], 2 * P, P, "diff2")
+        sum_errors_on_vector(reads3, target_sb[1][:, :, P : 2 * P], 3 * P, P)
+
+        roots = keep.tile([P, HALVES, G], F32, name="roots")
+        nc.scalar.activation(roots[:], sums[:], ACT.Sqrt)
+        result = keep.tile([P, HALVES, G], F32, name="result")
+        nc.vector.tensor_tensor(result[:], roots[:], tol_sb[:], ALU.subtract)
+        nc.sync.dma_start(out.rearrange("(h p) g -> p h g", p=P), result[:])

@@ -42,11 +42,8 @@ def tile_attend_readerrors_kernel(tc, query, keys_words, keys_scales, size, vals
 
         q_raw = keep.tile([P, PACK, Q], F32, name="q_raw")
         nc.sync.dma_start(q_raw[:], query.rearrange("(p j) q -> p j q", j=PACK))
-        for quad in range(4):
-            nc.sync.dma_start(
-                key_scales[32 * quad : 32 * quad + 4, :].bitcast(I32),
-                keys_scales[0, 4 * quad : 4 * quad + 4, :].bitcast(I32),
-            )
+        for row in range(4):
+            nc.sync.dma_start(key_scales[row:P:32, :].bitcast(I32), keys_scales[0, row:16:4, :].bitcast(I32))
         size_sb = keep.tile([P, PACK], F32, name="size_sb")
         nc.sync.dma_start(size_sb[:], size.rearrange("o (p t) -> p (o t)", t=PACK))
         key_words = keep.tile([P, T], U32, name="key_words", align_bytes=64)
@@ -59,12 +56,11 @@ def tile_attend_readerrors_kernel(tc, query, keys_words, keys_scales, size, vals
         tol_sb = keep.tile([P, HALVES, G], F32, name="tol_sb")
         nc.sync.dma_start(val_rows[0][:], vals[0:P, :])
         nc.sync.dma_start(fw_sb[:], fw.rearrange("o (p t) -> p (o t)", t=PACK))
-        nc.sync.dma_start(val_rows[1][:], vals[P : 2 * P, :])
+        for c in range(1, CHUNKS):
+            nc.sync.dma_start(val_rows[c][:], vals[c * P : (c + 1) * P, :])
+        for k in range(2):
+            nc.sync.dma_start(target_sb[k][:], target_rows[:, :, k * E // 2 : (k + 1) * E // 2])
         nc.sync.dma_start(tol_sb[:], tol.rearrange("(h p) g -> p h g", p=P))
-        nc.sync.dma_start(val_rows[2][:], vals[2 * P : 3 * P, :])
-        nc.sync.dma_start(target_sb[0][:], target_rows[:, :, 0 : E // 2])
-        nc.sync.dma_start(val_rows[3][:], vals[3 * P : 4 * P, :])
-        nc.sync.dma_start(target_sb[1][:], target_rows[:, :, E // 2 : E])
 
         q_grouped = keep.tile([P, Q, PACK], BF16, name="q_grouped", align_bytes=64)
         nc.scalar.activation(
@@ -78,8 +74,10 @@ def tile_attend_readerrors_kernel(tc, query, keys_words, keys_scales, size, vals
 
         k_scales = keep.tile([P, I], U8, name="k_scales", align_bytes=64)
         nc.vector.tensor_copy(k_scales[:], key_scales[:].indirect(offsets[:]))
-        k_codes = keep.tile([P, I], U32, name="k_codes", align_bytes=64)
-        nc.vector.tensor_copy(k_codes[:], key_words[:].indirect(offsets[:]))
+        k_codes = [keep.tile([P, I // 2], U32, name="k_codes%d" % s, align_bytes=64) for s in range(2)]
+        half_list = [offsets[:, 0 : I // 32], offsets[:, I // 32 : I // 16]]
+        for s in range(2):
+            nc.vector.tensor_copy(k_codes[s][:], key_words[:].indirect(half_list[s]))
 
         size_bank = psum.tile([P, PACK, P], F32, name="size_bank")
         fw_bank = psum.tile([P, PACK, P], F32, name="fw_bank")
@@ -88,73 +86,79 @@ def tile_attend_readerrors_kernel(tc, query, keys_words, keys_scales, size, vals
         size_row = size_bank[:].rearrange("c t p -> c p t")
         fw_row = fw_bank[:].rearrange("c t p -> c p t")
 
-        def turn_and_quantize(rows, name, grouped_tag, codes_tag):
+        def by_place(ap):
+            return ap.rearrange("q (p t) -> q p t", t=PACK)
+
+        scores = [psum.tile([P, I], F32, name="scores", tag="sums", bufs=3) for h in range(HALVES)]
+        for s in range(2):
+            slots = slice(s * I // 2, (s + 1) * I // 2)
+            for h in range(HALVES):
+                cols = slice(h * P, (h + 1) * P)
+                nc.tensor.matmul_mx(
+                    out=scores[h][:, slots],
+                    lhsT=q_codes[:, cols].bitcast(FP8X4),
+                    lhsT_scale=q_scales[:, cols],
+                    rhs=k_codes[s][:].bitcast(FP8X4),
+                    rhs_scale=k_scales[:, slots],
+                    start=True,
+                    stop=True,
+                )
+        w_rows = []
+        for h in range(HALVES):
+            neg_max = work.tile([P, 1], F32, name="neg_max")
+            nc.vector.tensor_reduce(neg_max[:], scores[h][:], AXIS.X, ALU.max, negate=True)
+            probs = work.tile([P, I], F32, name="probs")
+            row_sum = work.tile([P, 1], F32, name="row_sum")
+            nc.scalar.activation(probs[:], scores[h][:], ACT.Exp, bias=neg_max[:], scale=1.0, accum_out=row_sum[:])
+            inv_sum = work.tile([P, 1], F32, name="inv_sum")
+            nc.vector.reciprocal(inv_sum[:], row_sum[:])
+            w_half = work.tile([P, I], BF16, name="w_half")
+            nc.vector.scalar_tensor_tensor(by_place(w_half[:]), by_place(probs[:]), inv_sum[:], size_row, ALU.mult, ALU.mult)
+            w_rows.append(w_half)
+
+        v_rows = [keep.tile([P, I], BF16, name="v_rows%d" % c) for c in range(CHUNKS)]
+
+        def gather_on_both(c):
+            nc.scalar.activation(v_rows[c][:, 0 : I // 2], val_rows[c][:].indirect(half_list[0]), ACT.Copy)
+            nc.vector.tensor_copy(v_rows[c][:, I // 2 : I], val_rows[c][:].indirect(half_list[1]))
+
+        gather_on_both(0)
+        nc.scalar.activation(v_rows[1][:], val_rows[1][:].indirect(offsets[:]), ACT.Copy)
+        gather_on_both(2)
+
+        def turn_and_quantize(rows, name, grouped, copy):
             n = len(rows)
             turned = psum.tile([P, n, 2, P], F32, name="turned", tag="turned", bufs=3)
             for k in range(n):
                 words = rows[k][:].bitcast(F32)
                 for u in range(2):
                     nc.tensor.transpose(turned[:, k, u, :], words[:, u : I // 2 : 2], ident[:])
-            grouped = keep.tile([P, n * P * PACK], BF16, name=name + "_grouped", tag=grouped_tag, align_bytes=64)
-            nc.scalar.copy(
-                grouped[:].bitcast(F32).rearrange("p (k r u) -> p k r u", k=n, u=2),
+            copy(
+                grouped.bitcast(F32).rearrange("p (k r u) -> p k r u", k=n, u=2),
                 turned[:].rearrange("p k u r -> p k r u"),
             )
-            codes = keep.tile([P, n * P], U32, name=name + "_codes", tag=codes_tag, align_bytes=64)
+            codes = keep.tile([P, n * P], U32, name=name + "_codes", align_bytes=64)
             scales = keep.tile([P, n * P], U8, name=name + "_scales", align_bytes=64)
-            nc.vector.quantize_mx(codes[:].bitcast(FP8X4), scales[:], grouped[:])
+            nc.vector.quantize_mx(codes[:].bitcast(FP8X4), scales[:], grouped)
             return codes, scales
 
-        v_rows = [keep.tile([P, I], BF16, name="v_rows%d" % c) for c in range(CHUNKS)]
-        nc.scalar.activation(v_rows[0][:], val_rows[0][:].indirect(offsets[:]), ACT.Copy)
-
-        w_rows = []
-        for h in range(HALVES):
-            cols = slice(h * P, (h + 1) * P)
-            scores = psum.tile([P, I], F32, name="scores", tag="sums", bufs=3)
-            nc.tensor.matmul_mx(
-                out=scores[:],
-                lhsT=q_codes[:, cols].bitcast(FP8X4),
-                lhsT_scale=q_scales[:, cols],
-                rhs=k_codes[:].bitcast(FP8X4),
-                rhs_scale=k_scales[:],
-                start=True,
-                stop=True,
-            )
-            neg_max = work.tile([P, 1], F32, name="neg_max")
-            nc.vector.tensor_reduce(neg_max[:], scores[:], AXIS.X, ALU.max, negate=True)
-            probs = keep.tile([P, I], F32, name="probs%d" % h, tag="val0" if h == 0 else "probs", align_bytes=64)
-            row_sum = work.tile([P, 1], F32, name="row_sum")
-            nc.scalar.activation(probs[:], scores[:], ACT.Exp, bias=neg_max[:], scale=1.0, accum_out=row_sum[:])
-            inv_sum = work.tile([P, 1], F32, name="inv_sum")
-            nc.vector.reciprocal(inv_sum[:], row_sum[:])
-            w_half = work.tile([P, I], BF16, name="w_half")
-            nc.vector.scalar_tensor_tensor(
-                w_half[:].rearrange("q (p t) -> q p t", t=PACK),
-                probs[:].rearrange("q (p t) -> q p t", t=PACK),
-                inv_sum[:],
-                size_row,
-                ALU.mult,
-                ALU.mult,
-            )
-            w_rows.append(w_half)
-
-        nc.scalar.activation(v_rows[1][:], val_rows[1][:].indirect(offsets[:]), ACT.Copy)
-        nc.vector.tensor_copy(v_rows[2][:], val_rows[2][:].indirect(offsets[:]))
-        w_codes, w_scales = turn_and_quantize(w_rows, "w", "val1", "val2")
+        staged = keep.tile([P, 4 * I], BF16, name="staged", tag="val2", align_bytes=64)
+        w_first = turn_and_quantize([w_rows[0]], "w0", staged[:, 0:I], nc.vector.tensor_copy)
+        v_early = turn_and_quantize(v_rows[0:2], "v01", staged[:, 2 * I : 4 * I], nc.scalar.copy)
+        w_second = turn_and_quantize([w_rows[1]], "w1", staged[:, I : 2 * I], nc.vector.tensor_copy)
+        weights = [w_first, w_second]
         for t in range(PACK):
             nc.tensor.transpose(fw_bank[:, t, :], fw_sb[:, t : t + 1].to_broadcast([P, P]), ident[:])
 
-        def read_values(chunks):
-            name = "v%d" % chunks[0]
-            v_codes, v_scales = turn_and_quantize([v_rows[c] for c in chunks], name, name + "g", name + "c")
-            reads = psum.tile([P, HALVES, len(chunks) * P], F32, name="reads", tag="sums", bufs=3)
-            for h in range(HALVES):
-                cols = slice(h * P, (h + 1) * P)
+        def read_values(values, halves):
+            v_codes, v_scales = values
+            reads = psum.tile([P, len(halves), v_scales.shape[1]], F32, name="reads", tag="sums", bufs=3)
+            for k, h in enumerate(halves):
+                w_codes, w_scales = weights[h]
                 nc.tensor.matmul_mx(
-                    out=reads[:, h, :],
-                    lhsT=w_codes[:, cols].bitcast(FP8X4),
-                    lhsT_scale=w_scales[:, cols],
+                    out=reads[:, k, :],
+                    lhsT=w_codes[:].bitcast(FP8X4),
+                    lhsT_scale=w_scales[:],
                     rhs=v_codes[:].bitcast(FP8X4),
                     rhs_scale=v_scales[:],
                     start=True,
@@ -162,52 +166,46 @@ def tile_attend_readerrors_kernel(tc, query, keys_words, keys_scales, size, vals
                 )
             return reads
 
-        sums = keep.tile([P, HALVES, G], F32, name="sums")
+        reads_early = [read_values(v_early, [h]) for h in range(HALVES)]
+        staged_late = keep.tile([P, 2 * I], BF16, name="staged_late", align_bytes=64)
+        v_third = turn_and_quantize([v_rows[2]], "v2", staged_late[:, 0:I], nc.scalar.copy)
+        gather_on_both(3)
+        v_last = turn_and_quantize([v_rows[3]], "v3", staged_late[:, I : 2 * I], nc.scalar.copy)
 
-        def by_place(ap):
-            return ap.rearrange("q (p t) -> q p t", t=PACK)
+        sums = keep.tile([P, HALVES, G], F32, name="sums")
+        diff = keep.tile([P, HALVES, E], F32, name="diff")
+        squares = keep.tile([P, HALVES, E], F32, name="squares")
 
         def fw_at(first, width):
             return fw_row[:, first // PACK : (first + width) // PACK, :]
 
-        def sum_errors(reads, wanted, first, width, diff_tag):
-            diff = keep.tile([P, HALVES, width], F32, name="diff%d" % first, tag=diff_tag, align_bytes=64)
-            nc.vector.tensor_tensor(diff[:], reads[:], wanted, ALU.subtract)
-            squares = keep.tile([P, HALVES, width], F32, name="squares%d" % first)
-            nc.scalar.activation(squares[:], diff[:], ACT.Square)
-            for h in range(HALVES):
-                for e in range(0, width, BLOCK):
-                    g = (first + e) // BLOCK
-                    block = by_place(squares[:, h, e : e + BLOCK])
-                    nc.vector.scalar_tensor_tensor(
-                        block, block, 256.0 / BLOCK, fw_at(first + e, BLOCK), ALU.mult, ALU.mult,
-                        accum_out=sums[:, h, g : g + 1],
-                    )
+        def sum_blocks(h, first, width, factor):
+            for e in range(first, first + width, BLOCK):
+                block = by_place(squares[:, h, e : e + BLOCK])
+                nc.vector.scalar_tensor_tensor(
+                    block, block, 256.0 / BLOCK, factor(h, e), ALU.mult, ALU.mult,
+                    accum_out=sums[:, h, e // BLOCK : e // BLOCK + 1],
+                )
 
-        def sum_errors_on_vector(reads, wanted, first, width):
-            diff = keep.tile([P, HALVES, width], F32, name="diff_last")
-            weighted = keep.tile([P, HALVES, width], F32, name="weighted")
-            for h in range(HALVES):
-                nc.vector.tensor_tensor(diff[:, h, :], reads[:, h, :], wanted[:, h, :], ALU.subtract)
-            for h in range(HALVES):
-                nc.vector.tensor_tensor(by_place(weighted[:, h, :]), by_place(diff[:, h, :]), fw_at(first, width), ALU.mult)
-            for h in range(HALVES):
-                for e in range(0, width, BLOCK):
-                    g = (first + e) // BLOCK
-                    block = weighted[:, h, e : e + BLOCK]
-                    nc.vector.scalar_tensor_tensor(
-                        block, block, 256.0 / BLOCK, diff[:, h, e : e + BLOCK], ALU.mult, ALU.mult,
-                        accum_out=sums[:, h, g : g + 1],
-                    )
-
-        reads01 = read_values([0, 1])
-        reads2 = read_values([2])
-        nc.scalar.activation(v_rows[3][:, 0 : I // 2], val_rows[3][:].indirect(offsets[:, 0 : I // 32]), ACT.Copy)
-        nc.vector.tensor_copy(v_rows[3][:, I // 2 : I], val_rows[3][:].indirect(offsets[:, I // 32 : I // 16]))
-        reads3 = read_values([3])
-        sum_errors(reads01, target_sb[0][:], 0, 2 * P, "val3")
-        sum_errors(reads2, target_sb[1][:, :, 0:P], 2 * P, P, "diff2")
-        sum_errors_on_vector(reads3, target_sb[1][:, :, P : 2 * P], 3 * P, P)
+        early, third, last = slice(0, 2 * P), slice(2 * P, 3 * P), slice(3 * P, 4 * P)
+        for h in range(HALVES):
+            nc.vector.tensor_tensor(diff[:, h, early], reads_early[h][:, 0, :], target_sb[0][:, h, :], ALU.subtract)
+        reads_third = read_values(v_third, [0, 1])
+        reads_last = read_values(v_last, [0, 1])
+        for h in range(HALVES):
+            nc.scalar.activation(squares[:, h, early], diff[:, h, early], ACT.Square)
+        for h in range(HALVES):
+            sum_blocks(h, 0, 2 * P, lambda h, e: fw_at(e, BLOCK))
+        nc.vector.tensor_tensor(diff[:, :, third], reads_third[:], target_sb[1][:, :, 0:P], ALU.subtract)
+        nc.scalar.activation(squares[:, :, third], diff[:, :, third], ACT.Square)
+        for h in range(HALVES):
+            sum_blocks(h, 2 * P, P, lambda h, e: fw_at(e, BLOCK))
+        for h in range(HALVES):
+            nc.vector.tensor_tensor(diff[:, h, last], reads_last[:, h, :], target_sb[1][:, h, P : 2 * P], ALU.subtract)
+        for h in range(HALVES):
+            nc.vector.tensor_tensor(by_place(squares[:, h, last]), by_place(diff[:, h, last]), fw_at(3 * P, P), ALU.mult)
+        for h in range(HALVES):
+            sum_blocks(h, 3 * P, P, lambda h, e: by_place(diff[:, h, e : e + BLOCK]))
 
         roots = keep.tile([P, HALVES, G], F32, name="roots")
         nc.scalar.activation(roots[:], sums[:], ACT.Sqrt)

@@ -30,18 +30,19 @@ def tile_attend_readerrors_kernel(tc, query, keys_words, keys_scales, size, vals
     with ExitStack() as ctx:
         keep = ctx.enter_context(tc.tile_pool(name="keep", bufs=1))
         work = ctx.enter_context(tc.tile_pool(name="work", bufs=2))
+        shared = ctx.enter_context(tc.tile_pool(name="shared", bufs=1))
         psum = ctx.enter_context(tc.psum_pool(name="psum", bufs=1))
 
         offsets = keep.tile([P, I // 16], U16, name="offsets")
-        nc.sync.dma_start(offsets[:], offs)
 
-        key_scales = keep.tile([P, T], U8, name="key_scales", align_bytes=64)
+        key_scales = keep.tile([P, T], U8, name="key_scales", tag="key_scales", align_bytes=64)
         nc.gpsimd.memset(key_scales[:].bitcast(I32), 0)
         ident = keep.tile([P, P], F32, name="ident")
         make_identity(nc, ident[:])
 
         q_raw = keep.tile([P, PACK, Q], F32, name="q_raw")
         nc.sync.dma_start(q_raw[:], query.rearrange("(p j) q -> p j q", j=PACK))
+        nc.sync.dma_start(offsets[:], offs)
         for row in range(4):
             nc.sync.dma_start(key_scales[row:P:32, :].bitcast(I32), keys_scales[0, row:16:4, :].bitcast(I32))
         size_sb = keep.tile([P, PACK], F32, name="size_sb")
@@ -49,8 +50,10 @@ def tile_attend_readerrors_kernel(tc, query, keys_words, keys_scales, size, vals
         key_words = keep.tile([P, T], U32, name="key_words", align_bytes=64)
         nc.sync.dma_start(key_words[:].bitcast(I32), keys_words[0].rearrange("p n t -> p (n t)").bitcast(I32))
 
-        val_rows = [keep.tile([P, T], F32, name="val_rows%d" % c, tag="val%d" % c, align_bytes=64) for c in range(CHUNKS)]
-        target_rows = target.rearrange("(h p) e -> p h e", p=P)
+        val_rows = [keep.tile([P, T], F32, name="val_rows%d" % c, tag="val%d" % c, align_bytes=64) for c in (0, 1, 3)]
+        val_third = shared.tile([P, T], F32, name="val_third", offset=0)
+        val_rows = val_rows[0:2] + [val_third] + val_rows[2:]
+        target_rows = target.rearrange("(p h) e -> p h e", h=HALVES)
         target_sb = [keep.tile([P, HALVES, E // 2], F32, name="target%d" % k) for k in range(2)]
         fw_sb = keep.tile([P, PACK], F32, name="fw_sb")
         tol_sb = keep.tile([P, HALVES, G], F32, name="tol_sb")
@@ -60,26 +63,25 @@ def tile_attend_readerrors_kernel(tc, query, keys_words, keys_scales, size, vals
             nc.sync.dma_start(val_rows[c][:], vals[c * P : (c + 1) * P, :])
         for k in range(2):
             nc.sync.dma_start(target_sb[k][:], target_rows[:, :, k * E // 2 : (k + 1) * E // 2])
-        nc.sync.dma_start(tol_sb[:], tol.rearrange("(h p) g -> p h g", p=P))
-
-        q_grouped = keep.tile([P, Q, PACK], BF16, name="q_grouped", align_bytes=64)
-        nc.scalar.activation(
-            q_grouped[:].rearrange("p (c i) t -> p c t i", i=4),
-            q_raw[:].rearrange("p t (c i) -> p c t i", i=4),
-            ACT.Copy,
-        )
-        q_codes = keep.tile([P, Q], U32, name="q_codes", align_bytes=64)
-        q_scales = keep.tile([P, Q], U8, name="q_scales", align_bytes=64)
-        nc.vector.quantize_mx(q_codes[:].bitcast(FP8X4), q_scales[:], q_grouped[:].rearrange("p q t -> p (q t)"))
+        nc.sync.dma_start(tol_sb[:], tol.rearrange("(p h) g -> p h g", h=HALVES))
 
         k_scales = keep.tile([P, I], U8, name="k_scales", align_bytes=64)
         nc.vector.tensor_copy(k_scales[:], key_scales[:].indirect(offsets[:]))
+        q_grouped = keep.tile([P, Q, PACK], BF16, name="q_grouped", align_bytes=64)
+        nc.scalar.copy(
+            q_grouped[:].rearrange("p (h c i) t -> p c t i h", h=HALVES, i=2),
+            q_raw[:].rearrange("p t (c i h) -> p c t i h", h=HALVES, i=2),
+        )
+        q_codes = keep.tile([P, Q], U32, name="q_codes", tag="key_scales", align_bytes=64)
+        q_scales = keep.tile([P, Q], U8, name="q_scales", align_bytes=64)
+        nc.vector.quantize_mx(q_codes[:].bitcast(FP8X4), q_scales[:], q_grouped[:].rearrange("p q t -> p (q t)"))
+
         k_codes = [keep.tile([P, I // 2], U32, name="k_codes%d" % s, align_bytes=64) for s in range(2)]
         half_list = [offsets[:, 0 : I // 32], offsets[:, I // 32 : I // 16]]
         for s in range(2):
             nc.vector.tensor_copy(k_codes[s][:], key_words[:].indirect(half_list[s]))
 
-        size_bank = psum.tile([P, PACK, P], F32, name="size_bank")
+        size_bank = psum.tile([P, PACK, P], F32, name="size_bank", tag="spare")
         fw_bank = psum.tile([P, PACK, P], F32, name="fw_bank")
         for t in range(PACK):
             nc.tensor.transpose(size_bank[:, t, :], size_sb[:, t : t + 1].to_broadcast([P, P]), ident[:])
@@ -89,7 +91,7 @@ def tile_attend_readerrors_kernel(tc, query, keys_words, keys_scales, size, vals
         def by_place(ap):
             return ap.rearrange("q (p t) -> q p t", t=PACK)
 
-        scores = [psum.tile([P, I], F32, name="scores", tag="sums", bufs=3) for h in range(HALVES)]
+        scores = [psum.tile([P, I], F32, name="scores", tag="sums", bufs=2) for h in range(HALVES)]
         for s in range(2):
             slots = slice(s * I // 2, (s + 1) * I // 2)
             for h in range(HALVES):
@@ -103,32 +105,31 @@ def tile_attend_readerrors_kernel(tc, query, keys_words, keys_scales, size, vals
                     start=True,
                     stop=True,
                 )
+        v_rows = [keep.tile([P, I], BF16, name="v_rows%d" % c) for c in range(CHUNKS)]
+        nc.scalar.activation(v_rows[0][:], val_rows[0][:].indirect(offsets[:]), ACT.Copy)
+        probs = keep.tile([P, HALVES, I], F32, name="probs", tag="val0", align_bytes=64)
         w_rows = []
         for h in range(HALVES):
             neg_max = work.tile([P, 1], F32, name="neg_max")
             nc.vector.tensor_reduce(neg_max[:], scores[h][:], AXIS.X, ALU.max, negate=True)
-            probs = work.tile([P, I], F32, name="probs")
             row_sum = work.tile([P, 1], F32, name="row_sum")
-            nc.scalar.activation(probs[:], scores[h][:], ACT.Exp, bias=neg_max[:], scale=1.0, accum_out=row_sum[:])
+            nc.scalar.activation(probs[:, h, :], scores[h][:], ACT.Exp, bias=neg_max[:], scale=1.0, accum_out=row_sum[:])
             inv_sum = work.tile([P, 1], F32, name="inv_sum")
             nc.vector.reciprocal(inv_sum[:], row_sum[:])
             w_half = work.tile([P, I], BF16, name="w_half")
-            nc.vector.scalar_tensor_tensor(by_place(w_half[:]), by_place(probs[:]), inv_sum[:], size_row, ALU.mult, ALU.mult)
+            nc.vector.scalar_tensor_tensor(by_place(w_half[:]), by_place(probs[:, h, :]), inv_sum[:], size_row, ALU.mult, ALU.mult)
             w_rows.append(w_half)
-
-        v_rows = [keep.tile([P, I], BF16, name="v_rows%d" % c) for c in range(CHUNKS)]
 
         def gather_on_both(c):
             nc.scalar.activation(v_rows[c][:, 0 : I // 2], val_rows[c][:].indirect(half_list[0]), ACT.Copy)
             nc.vector.tensor_copy(v_rows[c][:, I // 2 : I], val_rows[c][:].indirect(half_list[1]))
 
-        gather_on_both(0)
         nc.scalar.activation(v_rows[1][:], val_rows[1][:].indirect(offsets[:]), ACT.Copy)
         gather_on_both(2)
 
-        def turn_and_quantize(rows, name, grouped, copy):
+        def turn_and_quantize(rows, name, grouped, codes, copy):
             n = len(rows)
-            turned = psum.tile([P, n, 2, P], F32, name="turned", tag="turned", bufs=3)
+            turned = psum.tile([P, n, 2, P], F32, name="turned", tag="turned", bufs=4)
             for k in range(n):
                 words = rows[k][:].bitcast(F32)
                 for u in range(2):
@@ -137,29 +138,31 @@ def tile_attend_readerrors_kernel(tc, query, keys_words, keys_scales, size, vals
                 grouped.bitcast(F32).rearrange("p (k r u) -> p k r u", k=n, u=2),
                 turned[:].rearrange("p k u r -> p k r u"),
             )
-            codes = keep.tile([P, n * P], U32, name=name + "_codes", align_bytes=64)
             scales = keep.tile([P, n * P], U8, name=name + "_scales", align_bytes=64)
-            nc.vector.quantize_mx(codes[:].bitcast(FP8X4), scales[:], grouped)
+            nc.vector.quantize_mx(codes.bitcast(FP8X4), scales[:], grouped)
             return codes, scales
 
-        staged = keep.tile([P, 4 * I], BF16, name="staged", tag="val2", align_bytes=64)
-        w_first = turn_and_quantize([w_rows[0]], "w0", staged[:, 0:I], nc.vector.tensor_copy)
-        v_early = turn_and_quantize(v_rows[0:2], "v01", staged[:, 2 * I : 4 * I], nc.scalar.copy)
-        w_second = turn_and_quantize([w_rows[1]], "w1", staged[:, I : 2 * I], nc.vector.tensor_copy)
+        staged = shared.tile([P, 3 * I], BF16, name="staged", align_bytes=64, offset=0)
+        codes_first = shared.tile([P, P], U32, name="codes_first", align_bytes=64, offset=4096)
+        staged_first = keep.tile([P, I], BF16, name="staged_first", align_bytes=64)
+        codes = keep.tile([P, 4 * P], U32, name="codes", align_bytes=64)
+        w_first = turn_and_quantize([w_rows[0]], "w0", staged_first[:], codes_first[:], nc.vector.tensor_copy)
+        v_early = turn_and_quantize(v_rows[0:2], "v01", staged[:, I : 3 * I], codes[:, 0 : 2 * P], nc.scalar.copy)
+        w_second = turn_and_quantize([w_rows[1]], "w1", staged[:, 0:I], codes[:, 2 * P : 3 * P], nc.vector.tensor_copy)
         weights = [w_first, w_second]
         for t in range(PACK):
             nc.tensor.transpose(fw_bank[:, t, :], fw_sb[:, t : t + 1].to_broadcast([P, P]), ident[:])
 
-        def read_values(values, halves):
+        def read_values(values, halves, tag="sums", bufs=2):
             v_codes, v_scales = values
-            reads = psum.tile([P, len(halves), v_scales.shape[1]], F32, name="reads", tag="sums", bufs=3)
+            reads = psum.tile([P, len(halves), v_scales.shape[1]], F32, name="reads", tag=tag, bufs=bufs)
             for k, h in enumerate(halves):
                 w_codes, w_scales = weights[h]
                 nc.tensor.matmul_mx(
                     out=reads[:, k, :],
-                    lhsT=w_codes[:].bitcast(FP8X4),
+                    lhsT=w_codes.bitcast(FP8X4),
                     lhsT_scale=w_scales[:],
-                    rhs=v_codes[:].bitcast(FP8X4),
+                    rhs=v_codes.bitcast(FP8X4),
                     rhs_scale=v_scales[:],
                     start=True,
                     stop=True,
@@ -167,10 +170,11 @@ def tile_attend_readerrors_kernel(tc, query, keys_words, keys_scales, size, vals
             return reads
 
         reads_early = [read_values(v_early, [h]) for h in range(HALVES)]
-        staged_late = keep.tile([P, 2 * I], BF16, name="staged_late", align_bytes=64)
-        v_third = turn_and_quantize([v_rows[2]], "v2", staged_late[:, 0:I], nc.scalar.copy)
         gather_on_both(3)
-        v_last = turn_and_quantize([v_rows[3]], "v3", staged_late[:, I : 2 * I], nc.scalar.copy)
+        codes_third = keep.tile([P, P], U32, name="codes_third", tag="val3", align_bytes=64)
+        staged_late = keep.tile([P, 2 * I], BF16, name="staged_late", align_bytes=64)
+        v_third = turn_and_quantize([v_rows[2]], "v2", staged_late[:, 0:I], codes_third[:], nc.scalar.copy)
+        v_last = turn_and_quantize([v_rows[3]], "v3", staged_late[:, I : 2 * I], codes[:, 3 * P :], nc.scalar.copy)
 
         sums = keep.tile([P, HALVES, G], F32, name="sums")
         diff = keep.tile([P, HALVES, E], F32, name="diff")
@@ -191,17 +195,17 @@ def tile_attend_readerrors_kernel(tc, query, keys_words, keys_scales, size, vals
         for h in range(HALVES):
             nc.vector.tensor_tensor(diff[:, h, early], reads_early[h][:, 0, :], target_sb[0][:, h, :], ALU.subtract)
         reads_third = read_values(v_third, [0, 1])
-        reads_last = read_values(v_last, [0, 1])
         for h in range(HALVES):
             nc.scalar.activation(squares[:, h, early], diff[:, h, early], ACT.Square)
+        nc.vector.tensor_tensor(diff[:, :, third], reads_third[:], target_sb[1][:, :, 0:P], ALU.subtract)
+        reads_last = [read_values(v_last, [0]), read_values(v_last, [1], "spare", 1)]
+        nc.scalar.activation(squares[:, :, third], diff[:, :, third], ACT.Square)
         for h in range(HALVES):
             sum_blocks(h, 0, 2 * P, lambda h, e: fw_at(e, BLOCK))
-        nc.vector.tensor_tensor(diff[:, :, third], reads_third[:], target_sb[1][:, :, 0:P], ALU.subtract)
-        nc.scalar.activation(squares[:, :, third], diff[:, :, third], ACT.Square)
         for h in range(HALVES):
             sum_blocks(h, 2 * P, P, lambda h, e: fw_at(e, BLOCK))
         for h in range(HALVES):
-            nc.vector.tensor_tensor(diff[:, h, last], reads_last[:, h, :], target_sb[1][:, h, P : 2 * P], ALU.subtract)
+            nc.vector.tensor_tensor(diff[:, h, last], reads_last[h][:, 0, :], target_sb[1][:, h, P : 2 * P], ALU.subtract)
         for h in range(HALVES):
             nc.vector.tensor_tensor(by_place(squares[:, h, last]), by_place(diff[:, h, last]), fw_at(3 * P, P), ALU.mult)
         for h in range(HALVES):
@@ -211,4 +215,4 @@ def tile_attend_readerrors_kernel(tc, query, keys_words, keys_scales, size, vals
         nc.scalar.activation(roots[:], sums[:], ACT.Sqrt)
         result = keep.tile([P, HALVES, G], F32, name="result")
         nc.vector.tensor_tensor(result[:], roots[:], tol_sb[:], ALU.subtract)
-        nc.sync.dma_start(out.rearrange("(h p) g -> p h g", p=P), result[:])
+        nc.sync.dma_start(out.rearrange("(p h) g -> p h g", h=HALVES), result[:])

from contextlib import ExitStack

import concourse.mybir as mybir
from concourse.masks import make_identity

D, T, I, Q, E, G = 512, 2048, 512, 256, 512, 8
FLOPS = 2 * Q * I * D + 2 * Q * E * I

F32 = mybir.dt.float32
BF16 = mybir.dt.bfloat16
I32 = mybir.dt.int32
U32 = mybir.dt.uint32
U16 = mybir.dt.uint16
U8 = mybir.dt.uint8
FP8X4 = mybir.dt.float8_e4m3fn_x4
ALU = mybir.AluOpType
ACT = mybir.ActivationFunctionType
AXIS = mybir.AxisListType

P = 128
PACK = 4
HALVES = Q // P
CHUNKS = E // P
BLOCK = E // G
EARLY = (CHUNKS - 1) * P


def tile_attend_readerrors_kernel(tc, query, keys_words, keys_scales, size, vals, target, fw, tol, offs, out):
    nc = tc.nc
    with ExitStack() as ctx:
        keep = ctx.enter_context(tc.tile_pool(name="keep", bufs=1))
        work = ctx.enter_context(tc.tile_pool(name="work", bufs=2))
        shared = ctx.enter_context(tc.tile_pool(name="shared", bufs=1))
        psum = ctx.enter_context(tc.psum_pool(name="psum", bufs=1))

        offsets = keep.tile([P, I // 16], U16, name="offsets")

        key_scales = keep.tile([P, T], U8, name="key_scales", tag="key_scales", align_bytes=64)
        nc.gpsimd.memset(key_scales[:].bitcast(I32), 0)
        ident = keep.tile([P, P], F32, name="ident")
        make_identity(nc, ident[:])

        q_raw = keep.tile([P, PACK, Q], F32, name="q_raw")
        nc.sync.dma_start(q_raw[:], query.rearrange("(p j) q -> p j q", j=PACK))
        nc.sync.dma_start(offsets[:], offs)
        for row in range(4):
            nc.sync.dma_start(key_scales[row:P:32, :].bitcast(I32), keys_scales[0, row:16:4, :].bitcast(I32))
        size_sb = keep.tile([P, PACK], F32, name="size_sb")
        nc.sync.dma_start(size_sb[:], size.rearrange("o (p t) -> p (o t)", t=PACK))
        key_words = keep.tile([P, T], U32, name="key_words", align_bytes=64)
        nc.sync.dma_start(key_words[:].bitcast(I32), keys_words[0].rearrange("p n t -> p (n t)").bitcast(I32))

        val_rows = [keep.tile([P, T], F32, name="val_rows%d" % c, tag="val%d" % c, align_bytes=64) for c in (0, 1, 3)]
        val_third = shared.tile([P, T], F32, name="val_third", offset=0)
        val_rows = val_rows[0:2] + [val_third] + val_rows[2:]
        target_rows = target.rearrange("(p h) e -> p h e", h=HALVES)
        target_sb = [keep.tile([P, HALVES, E // 2], F32, name="target%d" % k) for k in range(2)]
        fw_sb = keep.tile([P, PACK], F32, name="fw_sb")
        tol_sb = keep.tile([P, HALVES, G], F32, name="tol_sb")
        nc.sync.dma_start(val_rows[0][:], vals[0:P, :])
        nc.sync.dma_start(fw_sb[:], fw.rearrange("o (p t) -> p (o t)", t=PACK))
        for c in range(1, CHUNKS):
            nc.sync.dma_start(val_rows[c][:], vals[c * P : (c + 1) * P, :])
        for k in range(2):
            nc.sync.dma_start(target_sb[k][:], target_rows[:, :, k * E // 2 : (k + 1) * E // 2])
        nc.sync.dma_start(tol_sb[:], tol.rearrange("(p h) g -> p h g", h=HALVES))

        k_scales = keep.tile([P, I], U8, name="k_scales", align_bytes=64)
        nc.vector.tensor_copy(k_scales[:], key_scales[:].indirect(offsets[:]))
        q_grouped = keep.tile([P, Q, PACK], BF16, name="q_grouped", align_bytes=64)
        nc.scalar.copy(
            q_grouped[:].rearrange("p (h c i) t -> p c t i h", h=HALVES, i=2),
            q_raw[:].rearrange("p t (c i h) -> p c t i h", h=HALVES, i=2),
        )
        q_codes = keep.tile([P, Q], U32, name="q_codes", tag="key_scales", align_bytes=64)
        q_scales = keep.tile([P, Q], U8, name="q_scales", align_bytes=64)
        nc.vector.quantize_mx(q_codes[:].bitcast(FP8X4), q_scales[:], q_grouped[:].rearrange("p q t -> p (q t)"))

        k_codes = [keep.tile([P, I // 2], U32, name="k_codes%d" % s, align_bytes=64) for s in range(2)]
        half_list = [offsets[:, 0 : I // 32], offsets[:, I // 32 : I // 16]]
        for s in range(2):
            nc.vector.tensor_copy(k_codes[s][:], key_words[:].indirect(half_list[s]))

        size_bank = psum.tile([P, PACK, P], F32, name="size_bank", tag="spare")
        fw_bank = psum.tile([P, PACK, P], F32, name="fw_bank")
        for t in range(PACK):
            nc.tensor.transpose(size_bank[:, t, :], size_sb[:, t : t + 1].to_broadcast([P, P]), ident[:])
        size_row = size_bank[:].rearrange("c t p -> c p t")
        fw_row = fw_bank[:].rearrange("c t p -> c p t")

        def by_place(ap):
            return ap.rearrange("q (p t) -> q p t", t=PACK)

        scores = [psum.tile([P, I], F32, name="scores", tag="sums", bufs=2) for h in range(HALVES)]
        for s in range(2):
            slots = slice(s * I // 2, (s + 1) * I // 2)
            for h in range(HALVES):
                cols = slice(h * P, (h + 1) * P)
                nc.tensor.matmul_mx(
                    out=scores[h][:, slots],
                    lhsT=q_codes[:, cols].bitcast(FP8X4),
                    lhsT_scale=q_scales[:, cols],
                    rhs=k_codes[s][:].bitcast(FP8X4),
                    rhs_scale=k_scales[:, slots],
                    start=True,
                    stop=True,
                )
        v_rows = [keep.tile([P, I], BF16, name="v_rows%d" % c) for c in range(CHUNKS)]
        nc.scalar.activation(v_rows[0][:], val_rows[0][:].indirect(offsets[:]), ACT.Copy)
        probs = keep.tile([P, HALVES, I], F32, name="probs", tag="val0", align_bytes=64)
        w_rows = []
        for h in range(HALVES):
            neg_max = work.tile([P, 1], F32, name="neg_max")
            nc.vector.tensor_reduce(neg_max[:], scores[h][:], AXIS.X, ALU.max, negate=True)
            row_sum = work.tile([P, 1], F32, name="row_sum")
            nc.scalar.activation(probs[:, h, :], scores[h][:], ACT.Exp, bias=neg_max[:], scale=1.0, accum_out=row_sum[:])
            inv_sum = work.tile([P, 1], F32, name="inv_sum")
            nc.vector.reciprocal(inv_sum[:], row_sum[:])
            w_half = work.tile([P, I], BF16, name="w_half")
            nc.vector.scalar_tensor_tensor(by_place(w_half[:]), by_place(probs[:, h, :]), inv_sum[:], size_row, ALU.mult, ALU.mult)
            w_rows.append(w_half)

        def gather_on_both(c):
            nc.scalar.activation(v_rows[c][:, 0 : I // 2], val_rows[c][:].indirect(half_list[0]), ACT.Copy)
            nc.vector.tensor_copy(v_rows[c][:, I // 2 : I], val_rows[c][:].indirect(half_list[1]))

        nc.scalar.activation(v_rows[1][:], val_rows[1][:].indirect(offsets[:]), ACT.Copy)
        gather_on_both(2)

        def turn_and_quantize(rows, name, grouped, codes, copy):
            n = len(rows)
            turned = psum.tile([P, n, 2, P], F32, name="turned", tag="turned", bufs=4)
            for k in range(n):
                words = rows[k][:].bitcast(F32)
                for u in range(2):
                    nc.tensor.transpose(turned[:, k, u, :], words[:, u : I // 2 : 2], ident[:])
            copy(
                grouped.bitcast(F32).rearrange("p (k r u) -> p k r u", k=n, u=2),
                turned[:].rearrange("p k u r -> p k r u"),
            )
            scales = keep.tile([P, n * P], U8, name=name + "_scales", align_bytes=64)
            nc.vector.quantize_mx(codes.bitcast(FP8X4), scales[:], grouped)
            return codes, scales

        staged = shared.tile([P, 3 * I], BF16, name="staged", align_bytes=64, offset=0)
        codes_first = shared.tile([P, P], U32, name="codes_first", align_bytes=64, offset=4096)
        staged_first = keep.tile([P, I], BF16, name="staged_first", align_bytes=64)
        codes = keep.tile([P, 4 * P], U32, name="codes", align_bytes=64)
        w_first = turn_and_quantize([w_rows[0]], "w0", staged_first[:], codes_first[:], nc.vector.tensor_copy)
        v_early = turn_and_quantize(v_rows[0:2], "v01", staged[:, I : 3 * I], codes[:, 0 : 2 * P], nc.scalar.copy)
        w_second = turn_and_quantize([w_rows[1]], "w1", staged[:, 0:I], codes[:, 2 * P : 3 * P], nc.vector.tensor_copy)
        weights = [w_first, w_second]
        for t in range(PACK):
            nc.tensor.transpose(fw_bank[:, t, :], fw_sb[:, t : t + 1].to_broadcast([P, P]), ident[:])

        def read_values(values, halves, tag="sums", bufs=2):
            v_codes, v_scales = values
            reads = psum.tile([P, len(halves), v_scales.shape[1]], F32, name="reads", tag=tag, bufs=bufs)
            for k, h in enumerate(halves):
                w_codes, w_scales = weights[h]
                nc.tensor.matmul_mx(
                    out=reads[:, k, :],
                    lhsT=w_codes.bitcast(FP8X4),
                    lhsT_scale=w_scales[:],
                    rhs=v_codes.bitcast(FP8X4),
                    rhs_scale=v_scales[:],
                    start=True,
                    stop=True,
                )
            return reads

        reads_early = [read_values(v_early, [h]) for h in range(HALVES)]
        gather_on_both(3)
        codes_third = keep.tile([P, P], U32, name="codes_third", tag="val3", align_bytes=64)
        staged_late = keep.tile([P, 2 * I], BF16, name="staged_late", align_bytes=64)
        v_third = turn_and_quantize([v_rows[2]], "v2", staged_late[:, 0:I], codes_third[:], nc.scalar.copy)
        v_last = turn_and_quantize([v_rows[3]], "v3", staged_late[:, I : 2 * I], codes[:, 3 * P :], nc.scalar.copy)

        sums = keep.tile([P, HALVES, G], F32, name="sums")
        diff = keep.tile([P, HALVES, E], F32, name="diff")
        squares = keep.tile([P, HALVES, E], F32, name="squares")

        def fw_at(first, width):
            return fw_row[:, first // PACK : (first + width) // PACK, :]

        def sum_blocks(h, first, width, factor):
            for e in range(first, first + width, BLOCK):
                block = by_place(squares[:, h, e : e + BLOCK])
                nc.vector.scalar_tensor_tensor(
                    block, block, 256.0 / BLOCK, factor(h, e), ALU.mult, ALU.mult,
                    accum_out=sums[:, h, e // BLOCK : e // BLOCK + 1],
                )

        early, third, last = slice(0, 2 * P), slice(2 * P, 3 * P), slice(3 * P, 4 * P)
        for h in range(HALVES):
            nc.vector.tensor_tensor(diff[:, h, early], reads_early[h][:, 0, :], target_sb[0][:, h, :], ALU.subtract)
        reads_third = read_values(v_third, [0, 1])
        for h in range(HALVES):
            nc.scalar.activation(squares[:, h, early], diff[:, h, early], ACT.Square)
        nc.vector.tensor_tensor(diff[:, :, third], reads_third[:], target_sb[1][:, :, 0:P], ALU.subtract)
        reads_last = [read_values(v_last, [0]), read_values(v_last, [1], "spare", 1)]
        nc.scalar.activation(squares[:, :, third], diff[:, :, third], ACT.Square)
        for h in range(HALVES):
            sum_blocks(h, 0, 2 * P, lambda h, e: fw_at(e, BLOCK))
        for h in range(HALVES):
            sum_blocks(h, 2 * P, P, lambda h, e: fw_at(e, BLOCK))
        for h in range(HALVES):
            nc.vector.tensor_tensor(diff[:, h, last], reads_last[h][:, 0, :], target_sb[1][:, h, P : 2 * P], ALU.subtract)
        for h in range(HALVES):
            nc.vector.tensor_tensor(by_place(squares[:, h, last]), by_place(diff[:, h, last]), fw_at(3 * P, P), ALU.mult)
        for h in range(HALVES):
            sum_blocks(h, 3 * P, P, lambda h, e: by_place(diff[:, h, e : e + BLOCK]))

        roots = keep.tile([P, HALVES, G], F32, name="roots")
        nc.scalar.activation(roots[:], sums[:], ACT.Sqrt)
        result = keep.tile([P, HALVES, G], F32, name="result")
        nc.vector.tensor_tensor(result[:], roots[:], tol_sb[:], ALU.subtract)
        nc.sync.dma_start(out.rearrange("(p h) g -> p h g", h=HALVES), result[:])
